import numpy as np
import ml_dtypes


def mxq(x, axis, fmt="e4m3"):
    dtype, down = {"e4m3": (ml_dtypes.float8_e4m3fn, 7), "e5m2": (ml_dtypes.float8_e5m2, 14)}[fmt]
    v = np.moveaxis(np.asarray(x, np.float32).astype(ml_dtypes.bfloat16).astype(np.float64), axis, -1)
    blocks = v.reshape(v.shape[:-1] + (-1, 32))
    amax = np.abs(blocks).max(-1, keepdims=True)
    byte = np.maximum(np.where(amax > 0, np.frexp(amax)[1] - 1 + 127, 0) - down, 1)
    scale = np.exp2(byte - 127.0)
    codes = (blocks / scale).astype(np.float32).astype(dtype).astype(np.float64)
    return np.moveaxis((codes * scale).reshape(v.shape), -1, axis)


WIDE = False


def mx_kscale(k):
    if not WIDE:
        return np.ones(k)
    levels = np.array([30, -30])
    if k % 512:
        return np.exp2(np.random.permutation(np.resize(levels, k // 32))).repeat(32)
    a = np.empty((k // 512, 16))
    for p in range(k // 512):
        a[p, :8] = np.random.permutation(np.resize(levels, 8))
        for g in range(8):
            far = levels[np.abs(levels - a[p, g]) >= 10]
            a[p, g + 8] = far[np.random.randint(len(far))]
    return np.exp2(a.ravel()).repeat(32)


def f64(x):
    return np.asarray(x).astype(np.float64)


def striped(idx):
    return np.tile(np.asarray(idx).reshape(-1, 16).T, (8, 1)).astype(np.uint16)


def unstriped(offs):
    return offs[:16].T.reshape(-1).astype(np.int64)


E2M1 = np.array([0.0, 0.5, 1.0, 1.5, 2.0, 3.0, 4.0, 6.0, -0.0, -0.5, -1.0, -1.5, -2.0, -3.0, -4.0, -6.0])


def pack_weight(w, fmt):
    k, n = w.shape
    w = f64(np.asarray(w, np.float32).astype(ml_dtypes.bfloat16)).reshape(k // 32, 32, n)
    amax = np.abs(w).max(1)
    if fmt == "e4m3":
        byte = np.frexp(amax)[1] - 1 + 127 - 7
    else:
        mant, ex = np.frexp(amax / 6.0)
        byte = np.where(mant > 0.5, ex, ex - 1) + 127
    byte = np.clip(np.where(amax > 0, byte, 1), 1, 254)
    scaled = (w * np.exp2(127.0 - byte)[:, None, :]).reshape(k, n).astype(np.float32)
    by_word = np.ascontiguousarray(scaled.reshape(k // 512, 128, 4, n).transpose(0, 1, 3, 2))
    if fmt == "e4m3":
        words = by_word.astype(ml_dtypes.float8_e4m3fn).view(np.uint8)
    else:
        c = by_word.astype(ml_dtypes.float4_e2m1fn).view(np.uint8) & 0xF
        words = (c[..., 0::2] | (c[..., 1::2] << 4)).reshape(k // 512, 128, 2 * n)
    return np.ascontiguousarray(words), np.ascontiguousarray(byte.astype(np.uint8).reshape(k // 512, 16, n))


def unpack_weight(words, scales, fmt):
    g, _, n = scales.shape
    words = np.ascontiguousarray(words).reshape(g, 128, n, -1)
    if fmt == "e4m3":
        vals = words.view(ml_dtypes.float8_e4m3fn).astype(np.float64)
    else:
        nib = np.empty((g, 128, n, 4), np.uint8)
        nib[..., 0::2] = words & 0xF
        nib[..., 1::2] = words >> 4
        vals = E2M1[nib]
    vals = vals * np.repeat(np.exp2(scales.astype(np.float64) - 127.0), 8, axis=1)[..., None]
    return vals.transpose(0, 1, 3, 2).reshape(g * 512, n)


K, T, J, R, V, N = 1024, 512, 128, 512, 512, 256


def setup_inputs():
    n = np.random.standard_normal
    idx = np.random.permutation(T)[:J]
    idx2 = np.random.permutation(V)[:J]
    idx3 = np.random.permutation(V)[:J]
    fk = mx_kscale(K)
    fr = mx_kscale(R)
    xtp = pack_weight(n((K, T)) / fk[:, None], "e4m3")
    wbp = pack_weight(n((R, N)) * 1 / np.sqrt(R) / fr[:, None], "e2m1")
    return {
        "xt_words": xtp[0],
        "xt_scales": xtp[1],
        "w": (n((K, R)) * 1 / np.sqrt(K) * fk[:, None] * fr).astype(np.float32),
        "tb": (n((R, V)) * 0.7 * fr[:, None]).astype(np.float32),
        "wb_words": wbp[0],
        "wb_scales": wbp[1],
        "rs": (n((N, J))).astype(np.float32),
        "gm": (np.random.uniform(0.5, 2.0, (N, 1))).astype(np.float32),
        "offs": striped(idx),
        "offs2": striped(idx2),
        "offs3": striped(idx3),
    }


def reference(xt_words, xt_scales, w, tb, wb_words, wb_scales, rs, gm, offs, offs2, offs3):
    idx = unstriped(offs)
    idx2 = unstriped(offs2)
    idx3 = unstriped(offs3)
    xtu = unpack_weight(xt_words, xt_scales, "e4m3")
    wbu = unpack_weight(wb_words, wb_scales, "e2m1")
    wq = mxq(f64(w), 0, "e5m2")
    xtidxg = xtu[:, idx]
    a = wq.T @ xtidxg
    hid = np.maximum(a + f64(tb)[:, idx2] - f64(tb)[:, idx3], 0.0)
    hidq = mxq(hid, 0, "e5m2")
    p = wbu.T @ hidq
    y = f64(gm) * p + f64(rs)
    return y

@@ -1,0 +1,129 @@
+from contextlib import ExitStack
+
+import concourse.mybir as mybir
+
+K, T, J, R, V, N = 1024, 512, 128, 512, 512, 256
+FLOPS = 2 * K * R * J + 2 * R * N * J
+
+F32 = mybir.dt.float32
+BF16 = mybir.dt.bfloat16
+I32 = mybir.dt.int32
+U32 = mybir.dt.uint32
+U16 = mybir.dt.uint16
+U8 = mybir.dt.uint8
+E4M3 = mybir.dt.float8_e4m3fn_x4
+E5M2 = mybir.dt.float8_e5m2_x4
+E2M1 = mybir.dt.float4_e2m1fn_x4
+ALU = mybir.AluOpType
+ACT = mybir.ActivationFunctionType
+
+P = 128
+PACK = 4
+PASSES = K // (P * PACK)
+HALVES = N // P
+M_SCALAR = 48
+
+
+def tile_list_picked_tworeach_residual_kernel(tc, xt_words, xt_scales, w, tb, wb_words, wb_scales, rs, gm, offs, offs2, offs3, out):
+    nc = tc.nc
+    with ExitStack() as ctx:
+        keep = ctx.enter_context(tc.tile_pool(name="keep", bufs=1))
+        psum = ctx.enter_context(tc.psum_pool(name="psum", bufs=1))
+
+        idx = keep.tile([P, J // 16], U16, name="idx")
+        idx2 = keep.tile([P, J // 16], U16, name="idx2")
+        idx3 = keep.tile([P, J // 16], U16, name="idx3")
+        x_words = keep.tile([P, PASSES, T], I32, name="x_words", align_bytes=64)
+        x_scales = keep.tile([P, PASSES, T], U8, name="x_scales", align_bytes=64)
+        b_words = keep.tile([P, 2 * N], U8, name="b_words", align_bytes=64)
+        b_scales = keep.tile([P, N], U8, name="b_scales", align_bytes=64)
+        table = [keep.tile([P, V], F32, name=f"table{t}", align_bytes=64) for t in range(PACK)]
+        w_raw = [keep.tile([P, PACK, R], F32, name=f"w_raw{z}", align_bytes=64) for z in range(PASSES)]
+        res = keep.tile([P, HALVES, J], F32, name="res", align_bytes=64)
+        gain = keep.tile([P, HALVES, 1], F32, name="gain")
+
+        nc.vector.memset(x_scales[:].rearrange("p z c -> p (z c)").bitcast(I32), 0)
+        nc.vector.memset(b_scales[:].bitcast(I32), 0)
+
+        tb_rows = tb.rearrange("(p t) v -> p t v", t=PACK)
+        w_rows = w.rearrange("(z p j) r -> z p j r", z=PASSES, j=PACK)
+        nc.sync.dma_start(out=x_words[:], in_=xt_words.rearrange("z p c b -> p z (c b)").bitcast(I32))
+        nc.sync.dma_start(idx[:], offs)
+        nc.sync.dma_start(out=table[0][:], in_=tb_rows[:, 0, :])
+        nc.sync.dma_start(idx3[:], offs3)
+        nc.sync.dma_start(idx2[:], offs2)
+        nc.sync.dma_start(out=table[1][:], in_=tb_rows[:, 1, :])
+        nc.sync.dma_start(out=w_raw[0][:], in_=w_rows[0])
+        nc.sync.dma_start(out=w_raw[1][:], in_=w_rows[1])
+        nc.sync.dma_start(out=table[2][:], in_=tb_rows[:, 2, :])
+        nc.sync.dma_start(out=table[3][:], in_=tb_rows[:, 3, :])
+        nc.sync.dma_start(out=b_words[:].bitcast(I32), in_=wb_words[0].bitcast(I32))
+        nc.sync.dma_start(out=res[:], in_=rs.rearrange("(h p) j -> p h j", p=P))
+
+        xs_rows = xt_scales.rearrange("z q c -> q z c").bitcast(I32)
+        bs_rows = wb_scales[0].bitcast(I32)
+        for q in range(4):
+            nc.scalar.dma_start(out=x_scales[32 * q : 32 * q + 4, :, :].bitcast(I32), in_=xs_rows[4 * q : 4 * q + 4])
+        for q in range(4):
+            nc.gpsimd.dma_start(out=b_scales[32 * q : 32 * q + 4, :].bitcast(I32), in_=bs_rows[4 * q : 4 * q + 4])
+        with nc.allow_non_contiguous_dma(reason="one factor for each output row"):
+            nc.gpsimd.dma_start(out=gain[:], in_=gm.rearrange("(h p) o -> p h o", p=P))
+
+        xg_words = keep.tile([P, PASSES, J], U32, name="xg_words", align_bytes=64)
+        xg_scales = keep.tile([P, PASSES, J], U8, name="xg_scales", align_bytes=64)
+        for z in range(PASSES):
+            nc.vector.tensor_copy(xg_words[:, z, :], x_words[:, z, :].bitcast(U32).indirect(idx[:]))
+        for z in range(PASSES):
+            nc.vector.tensor_copy(xg_scales[:, z, :], x_scales[:, z, :].indirect(idx[:]))
+
+        taken = [keep.tile([P, J], F32, name=f"taken{t}", align_bytes=64) for t in range(PACK)]
+        diff = [keep.tile([P, J], F32, name=f"diff{t}", align_bytes=64) for t in range(PACK)]
+
+        def look_up(t):
+            nc.scalar.activation(taken[t][:], table[t][:].indirect(idx3[:]), ACT.Copy)
+            nc.vector.tensor_tensor(diff[t][:], table[t][:].indirect(idx2[:]), taken[t][:], ALU.subtract)
+
+        acc = [psum.tile([P, J], F32, name=f"acc{t}") for t in range(PACK)]
+
+        def first_product(z):
+            grouped = keep.tile([P, PACK, P, PACK], BF16, name=f"w_grouped{z}", align_bytes=64)
+            codes = keep.tile([P, R], U32, name=f"w_codes{z}", align_bytes=64)
+            scales = keep.tile([P, R], U8, name=f"w_scales{z}", align_bytes=64)
+            src = w_raw[z][:].rearrange("p j (m t) -> p m j t", t=PACK)
+            dst = grouped[:].rearrange("p t m j -> p m j t")
+            nc.scalar.copy(dst[:, :M_SCALAR], src[:, :M_SCALAR])
+            nc.vector.tensor_copy(dst[:, M_SCALAR:], src[:, M_SCALAR:])
+            for t in range(PACK):
+                cols = slice(t * P, (t + 1) * P)
+                nc.vector.quantize_mx(out=codes[:, cols].bitcast(E5M2), scales=scales[:, cols],
+                                      in_=grouped[:, t].rearrange("p m j -> p (m j)"))
+                nc.tensor.matmul_mx(out=acc[t][:], lhsT=codes[:, cols].bitcast(E5M2), lhsT_scale=scales[:, cols],
+                                    rhs=xg_words[:, z, :].bitcast(E4M3), rhs_scale=xg_scales[:, z, :],
+                                    start=(z == 0), stop=(z == PASSES - 1))
+
+        look_up(0)
+        look_up(1)
+        first_product(0)
+        first_product(1)
+        look_up(2)
+        look_up(3)
+
+        pre = keep.tile([P, PACK, J], F32, name="pre", align_bytes=64)
+        for t in range(PACK):
+            nc.vector.tensor_tensor(pre[:, t, :], acc[t][:], diff[t][:], ALU.add)
+        hid = keep.tile([P, J, PACK], BF16, name="hid", align_bytes=64)
+        nc.vector.tensor_scalar(hid[:].rearrange("p (c i) t -> p c t i", i=4), pre[:].rearrange("p t (c i) -> p c t i", i=4),
+                                0.0, None, ALU.max)
+        h_codes = keep.tile([P, J], U32, name="h_codes", align_bytes=64)
+        h_scales = keep.tile([P, J], U8, name="h_scales", align_bytes=64)
+        nc.vector.quantize_mx(out=h_codes[:].bitcast(E5M2), scales=h_scales[:], in_=hid[:].rearrange("p j t -> p (j t)"))
+
+        queues = [nc.sync, nc.scalar]
+        for h in range(HALVES):
+            prod = psum.tile([P, J], F32, name=f"prod{h}")
+            nc.tensor.matmul_mx(out=prod[:], lhsT=b_words[:, 2 * P * h : 2 * P * (h + 1)].bitcast(E2M1),
+                                lhsT_scale=b_scales[:, P * h : P * (h + 1)],
+                                rhs=h_codes[:].bitcast(E5M2), rhs_scale=h_scales[:], start=True, stop=True)
+            result = keep.tile([P, J], F32, name=f"result{h}", align_bytes=64)
+            nc.vector.scalar_tensor_tensor(result[:], prod[:], gain[:, h, :], res[:, h, :], ALU.mult, ALU.add)
+            queues[h].dma_start(out=out[P * h : P * (h + 1), :], in_=result[:])

@@ -21,7 +21,7 @@ P = 128
 PACK = 4
 PASSES = K // (P * PACK)
 HALVES = N // P
-M_SCALAR = 48
+M_SCALAR = 44
 
 
 def tile_list_picked_tworeach_residual_kernel(tc, xt_words, xt_scales, w, tb, wb_words, wb_scales, rs, gm, offs, offs2, offs3, out):
@@ -47,76 +47,99 @@ def tile_list_picked_tworeach_residual_kernel(tc, xt_words, xt_scales, w, tb, wb
 
         tb_rows = tb.rearrange("(p t) v -> p t v", t=PACK)
         w_rows = w.rearrange("(z p j) r -> z p j r", z=PASSES, j=PACK)
-        nc.sync.dma_start(out=x_words[:], in_=xt_words.rearrange("z p c b -> p z (c b)").bitcast(I32))
+        xw_rows = xt_words.rearrange("z p c b -> p z (c b)").bitcast(I32)
+        xs_rows = xt_scales.rearrange("z q c -> q z c").bitcast(I32)
+        bs_rows = wb_scales[0].bitcast(I32)
+
+        def load_b_scales(q):
+            nc.sync.dma_start(out=b_scales[32 * q : 32 * q + 4, :].bitcast(I32), in_=bs_rows[4 * q : 4 * q + 4])
+
+        nc.sync.dma_start(out=x_words[:], in_=xw_rows)
+        for q in range(4):
+            nc.sync.dma_start(out=x_scales[32 * q : 32 * q + 4, :, :].bitcast(I32), in_=xs_rows[4 * q : 4 * q + 4])
         nc.sync.dma_start(idx[:], offs)
-        nc.sync.dma_start(out=table[0][:], in_=tb_rows[:, 0, :])
+        nc.sync.dma_start(out=w_raw[0][:], in_=w_rows[0])
         nc.sync.dma_start(idx3[:], offs3)
         nc.sync.dma_start(idx2[:], offs2)
+        nc.sync.dma_start(out=table[0][:], in_=tb_rows[:, 0, :])
         nc.sync.dma_start(out=table[1][:], in_=tb_rows[:, 1, :])
-        nc.sync.dma_start(out=w_raw[0][:], in_=w_rows[0])
         nc.sync.dma_start(out=w_raw[1][:], in_=w_rows[1])
         nc.sync.dma_start(out=table[2][:], in_=tb_rows[:, 2, :])
         nc.sync.dma_start(out=table[3][:], in_=tb_rows[:, 3, :])
+        load_b_scales(0)
+        load_b_scales(1)
+        load_b_scales(2)
+        load_b_scales(3)
         nc.sync.dma_start(out=b_words[:].bitcast(I32), in_=wb_words[0].bitcast(I32))
+        with nc.allow_non_contiguous_dma(reason="one factor for each output row"):
+            nc.sync.dma_start(out=gain[:], in_=gm.rearrange("(h p) o -> p h o", p=P))
         nc.sync.dma_start(out=res[:], in_=rs.rearrange("(h p) j -> p h j", p=P))
 
-        xs_rows = xt_scales.rearrange("z q c -> q z c").bitcast(I32)
-        bs_rows = wb_scales[0].bitcast(I32)
-        for q in range(4):
-            nc.scalar.dma_start(out=x_scales[32 * q : 32 * q + 4, :, :].bitcast(I32), in_=xs_rows[4 * q : 4 * q + 4])
-        for q in range(4):
-            nc.gpsimd.dma_start(out=b_scales[32 * q : 32 * q + 4, :].bitcast(I32), in_=bs_rows[4 * q : 4 * q + 4])
-        with nc.allow_non_contiguous_dma(reason="one factor for each output row"):
-            nc.gpsimd.dma_start(out=gain[:], in_=gm.rearrange("(h p) o -> p h o", p=P))
+        xg_words = [keep.tile([P, J], U32, name=f"xg_words{z}", align_bytes=64) for z in range(PASSES)]
+        xg_scales = [keep.tile([P, J], U8, name=f"xg_scales{z}", align_bytes=64) for z in range(PASSES)]
+        grouped = [keep.tile([P, PACK, P, PACK], BF16, name=f"w_grouped{z}", align_bytes=64) for z in range(PASSES)]
+        codes = [keep.tile([P, R], U32, name=f"w_codes{z}", align_bytes=64) for z in range(PASSES)]
+        scales = [keep.tile([P, R], U8, name=f"w_scales{z}", align_bytes=64) for z in range(PASSES)]
+        acc = [psum.tile([P, 2, J], F32, name=f"acc{u}") for u in range(2)]
+        taken = [keep.tile([P, 2, J], F32, name=f"taken{u}", align_bytes=64) for u in range(2)]
+        given = keep.tile([P, 2, J], F32, name="given", align_bytes=64)
+        part = [keep.tile([P, 2, J], F32, name="part", align_bytes=64)]
+        pre = keep.tile([P, 2, PACK, J // 2], F32, name="pre", align_bytes=64)
+        upper = keep.tile([P, 2, 2, J // 2], F32, name="upper", align_bytes=64)
 
-        xg_words = keep.tile([P, PASSES, J], U32, name="xg_words", align_bytes=64)
-        xg_scales = keep.tile([P, PASSES, J], U8, name="xg_scales", align_bytes=64)
-        for z in range(PASSES):
-            nc.vector.tensor_copy(xg_words[:, z, :], x_words[:, z, :].bitcast(U32).indirect(idx[:]))
-        for z in range(PASSES):
-            nc.vector.tensor_copy(xg_scales[:, z, :], x_scales[:, z, :].indirect(idx[:]))
-
-        taken = [keep.tile([P, J], F32, name=f"taken{t}", align_bytes=64) for t in range(PACK)]
-        diff = [keep.tile([P, J], F32, name=f"diff{t}", align_bytes=64) for t in range(PACK)]
-
-        def look_up(t):
-            nc.scalar.activation(taken[t][:], table[t][:].indirect(idx3[:]), ACT.Copy)
-            nc.vector.tensor_tensor(diff[t][:], table[t][:].indirect(idx2[:]), taken[t][:], ALU.subtract)
-
-        acc = [psum.tile([P, J], F32, name=f"acc{t}") for t in range(PACK)]
-
-        def first_product(z):
-            grouped = keep.tile([P, PACK, P, PACK], BF16, name=f"w_grouped{z}", align_bytes=64)
-            codes = keep.tile([P, R], U32, name=f"w_codes{z}", align_bytes=64)
-            scales = keep.tile([P, R], U8, name=f"w_scales{z}", align_bytes=64)
-            src = w_raw[z][:].rearrange("p j (m t) -> p m j t", t=PACK)
-            dst = grouped[:].rearrange("p t m j -> p m j t")
+        def round_w(z, u):
+            src = w_raw[z][:].rearrange("p j (m t) -> p m j t", t=PACK)[:, :, :, 2 * u : 2 * u + 2]
+            dst = grouped[z][:, 2 * u : 2 * u + 2].rearrange("p t m j -> p m j t")
             nc.scalar.copy(dst[:, :M_SCALAR], src[:, :M_SCALAR])
             nc.vector.tensor_copy(dst[:, M_SCALAR:], src[:, M_SCALAR:])
-            for t in range(PACK):
-                cols = slice(t * P, (t + 1) * P)
-                nc.vector.quantize_mx(out=codes[:, cols].bitcast(E5M2), scales=scales[:, cols],
-                                      in_=grouped[:, t].rearrange("p m j -> p (m j)"))
-                nc.tensor.matmul_mx(out=acc[t][:], lhsT=codes[:, cols].bitcast(E5M2), lhsT_scale=scales[:, cols],
-                                    rhs=xg_words[:, z, :].bitcast(E4M3), rhs_scale=xg_scales[:, z, :],
-                                    start=(z == 0), stop=(z == PASSES - 1))
 
-        look_up(0)
-        look_up(1)
-        first_product(0)
-        first_product(1)
-        look_up(2)
-        look_up(3)
+        def first_product(z, u):
+            cols = slice(2 * u * P, 2 * (u + 1) * P)
+            nc.vector.quantize_mx(out=codes[z][:, cols].bitcast(E5M2), scales=scales[z][:, cols],
+                                  in_=grouped[z][:, 2 * u : 2 * u + 2].rearrange("p t m j -> p (t m j)"))
+            for i in range(2):
+                cols = slice((2 * u + i) * P, (2 * u + i + 1) * P)
+                nc.tensor.matmul_mx(out=acc[u][:, i, :], lhsT=codes[z][:, cols].bitcast(E5M2), lhsT_scale=scales[z][:, cols],
+                                    rhs=xg_words[z][:].bitcast(E4M3), rhs_scale=xg_scales[z][:],
+                                    start=(z == 0 and i == 0), stop=(z == PASSES - 1 and i == 1))
 
-        pre = keep.tile([P, PACK, J], F32, name="pre", align_bytes=64)
-        for t in range(PACK):
-            nc.vector.tensor_tensor(pre[:, t, :], acc[t][:], diff[t][:], ALU.add)
+        for z in range(PASSES):
+            nc.vector.tensor_copy(xg_words[z][:], x_words[:, z, :].bitcast(U32).indirect(idx[:]))
+        for z in range(PASSES):
+            nc.vector.tensor_copy(xg_scales[z][:], x_scales[:, z, :].indirect(idx[:]))
+        round_w(0, 0)
+        round_w(0, 1)
+        first_product(0, 0)
+        first_product(0, 1)
+        nc.scalar.activation(taken[0][:, 0, :], table[0][:].indirect(idx3[:]), ACT.Copy)
+        nc.vector.tensor_tensor(part[0][:, 0, :], table[0][:].indirect(idx2[:]), taken[0][:, 0, :], ALU.subtract)
+        nc.scalar.activation(taken[0][:, 1, :], table[1][:].indirect(idx3[:]), ACT.Copy)
+        nc.vector.tensor_tensor(part[0][:, 1, :], table[1][:].indirect(idx2[:]), taken[0][:, 1, :], ALU.subtract)
+        round_w(1, 1)
+        round_w(1, 0)
+        first_product(1, 1)
+        first_product(1, 0)
+        nc.scalar.activation(taken[1][:, 0, :], table[2][:].indirect(idx3[:]), ACT.Copy)
+        nc.scalar.activation(given[:, 0, :], table[2][:].indirect(idx2[:]), ACT.Copy)
+        nc.scalar.activation(taken[1][:, 1, :], table[3][:].indirect(idx3[:]), ACT.Copy)
+        nc.vector.tensor_copy(given[:, 1, :], table[3][:].indirect(idx2[:]))
+
         hid = keep.tile([P, J, PACK], BF16, name="hid", align_bytes=64)
-        nc.vector.tensor_scalar(hid[:].rearrange("p (c i) t -> p c t i", i=4), pre[:].rearrange("p t (c i) -> p c t i", i=4),
-                                0.0, None, ALU.max)
         h_codes = keep.tile([P, J], U32, name="h_codes", align_bytes=64)
         h_scales = keep.tile([P, J], U8, name="h_scales", align_bytes=64)
-        nc.vector.quantize_mx(out=h_codes[:].bitcast(E5M2), scales=h_scales[:], in_=hid[:].rearrange("p j t -> p (j t)"))
+        halves = [slice(h * J // 2, (h + 1) * J // 2) for h in range(2)]
+        for h, cols in enumerate(halves):
+            nc.vector.tensor_tensor(upper[:, h], acc[1][:, :, cols], given[:, :, cols], ALU.add)
+        for h, cols in enumerate(halves):
+            nc.vector.tensor_tensor(pre[:, h, 0:2, :], acc[0][:, :, cols], part[0][:, :, cols], ALU.add)
+        for h, cols in enumerate(halves):
+            nc.vector.tensor_tensor(pre[:, h, 2:4, :], upper[:, h], taken[1][:, :, cols], ALU.subtract)
+        for h, cols in enumerate(halves):
+            nc.vector.tensor_scalar(hid[:, cols, :].rearrange("p (c i) t -> p c t i", i=4),
+                                    pre[:, h].rearrange("p t (c i) -> p c t i", i=4), 0.0, None, ALU.max)
+        for cols in halves:
+            nc.vector.quantize_mx(out=h_codes[:, cols].bitcast(E5M2), scales=h_scales[:, cols],
+                                  in_=hid[:, cols, :].rearrange("p j t -> p (j t)"))
 
         queues = [nc.sync, nc.scalar]
         for h in range(HALVES):

from contextlib import ExitStack

import concourse.mybir as mybir

K, T, J, R, V, N = 1024, 512, 128, 512, 512, 256
FLOPS = 2 * K * R * J + 2 * R * N * J

F32 = mybir.dt.float32
BF16 = mybir.dt.bfloat16
I32 = mybir.dt.int32
U32 = mybir.dt.uint32
U16 = mybir.dt.uint16
U8 = mybir.dt.uint8
E4M3 = mybir.dt.float8_e4m3fn_x4
E5M2 = mybir.dt.float8_e5m2_x4
E2M1 = mybir.dt.float4_e2m1fn_x4
ALU = mybir.AluOpType
ACT = mybir.ActivationFunctionType

P = 128
PACK = 4
PASSES = K // (P * PACK)
HALVES = N // P
M_SCALAR = 44


def tile_list_picked_tworeach_residual_kernel(tc, xt_words, xt_scales, w, tb, wb_words, wb_scales, rs, gm, offs, offs2, offs3, out):
    nc = tc.nc
    with ExitStack() as ctx:
        keep = ctx.enter_context(tc.tile_pool(name="keep", bufs=1))
        psum = ctx.enter_context(tc.psum_pool(name="psum", bufs=1))

        idx = keep.tile([P, J // 16], U16, name="idx")
        idx2 = keep.tile([P, J // 16], U16, name="idx2")
        idx3 = keep.tile([P, J // 16], U16, name="idx3")
        x_words = keep.tile([P, PASSES, T], I32, name="x_words", align_bytes=64)
        x_scales = keep.tile([P, PASSES, T], U8, name="x_scales", align_bytes=64)
        b_words = keep.tile([P, 2 * N], U8, name="b_words", align_bytes=64)
        b_scales = keep.tile([P, N], U8, name="b_scales", align_bytes=64)
        table = [keep.tile([P, V], F32, name=f"table{t}", align_bytes=64) for t in range(PACK)]
        w_raw = [keep.tile([P, PACK, R], F32, name=f"w_raw{z}", align_bytes=64) for z in range(PASSES)]
        res = keep.tile([P, HALVES, J], F32, name="res", align_bytes=64)
        gain = keep.tile([P, HALVES, 1], F32, name="gain")

        nc.vector.memset(x_scales[:].rearrange("p z c -> p (z c)").bitcast(I32), 0)
        nc.vector.memset(b_scales[:].bitcast(I32), 0)

        tb_rows = tb.rearrange("(p t) v -> p t v", t=PACK)
        w_rows = w.rearrange("(z p j) r -> z p j r", z=PASSES, j=PACK)
        xw_rows = xt_words.rearrange("z p c b -> p z (c b)").bitcast(I32)
        xs_rows = xt_scales.rearrange("z q c -> q z c").bitcast(I32)
        bs_rows = wb_scales[0].bitcast(I32)

        def load_b_scales(q):
            nc.sync.dma_start(out=b_scales[32 * q : 32 * q + 4, :].bitcast(I32), in_=bs_rows[4 * q : 4 * q + 4])

        nc.sync.dma_start(out=x_words[:], in_=xw_rows)
        for q in range(4):
            nc.sync.dma_start(out=x_scales[32 * q : 32 * q + 4, :, :].bitcast(I32), in_=xs_rows[4 * q : 4 * q + 4])
        nc.sync.dma_start(idx[:], offs)
        nc.sync.dma_start(out=w_raw[0][:], in_=w_rows[0])
        nc.sync.dma_start(idx3[:], offs3)
        nc.sync.dma_start(idx2[:], offs2)
        nc.sync.dma_start(out=table[0][:], in_=tb_rows[:, 0, :])
        nc.sync.dma_start(out=table[1][:], in_=tb_rows[:, 1, :])
        nc.sync.dma_start(out=w_raw[1][:], in_=w_rows[1])
        nc.sync.dma_start(out=table[2][:], in_=tb_rows[:, 2, :])
        nc.sync.dma_start(out=table[3][:], in_=tb_rows[:, 3, :])
        load_b_scales(0)
        load_b_scales(1)
        load_b_scales(2)
        load_b_scales(3)
        nc.sync.dma_start(out=b_words[:].bitcast(I32), in_=wb_words[0].bitcast(I32))
        with nc.allow_non_contiguous_dma(reason="one factor for each output row"):
            nc.sync.dma_start(out=gain[:], in_=gm.rearrange("(h p) o -> p h o", p=P))
        nc.sync.dma_start(out=res[:], in_=rs.rearrange("(h p) j -> p h j", p=P))

        xg_words = [keep.tile([P, J], U32, name=f"xg_words{z}", align_bytes=64) for z in range(PASSES)]
        xg_scales = [keep.tile([P, J], U8, name=f"xg_scales{z}", align_bytes=64) for z in range(PASSES)]
        grouped = [keep.tile([P, PACK, P, PACK], BF16, name=f"w_grouped{z}", align_bytes=64) for z in range(PASSES)]
        codes = [keep.tile([P, R], U32, name=f"w_codes{z}", align_bytes=64) for z in range(PASSES)]
        scales = [keep.tile([P, R], U8, name=f"w_scales{z}", align_bytes=64) for z in range(PASSES)]
        acc = [psum.tile([P, 2, J], F32, name=f"acc{u}") for u in range(2)]
        taken = [keep.tile([P, 2, J], F32, name=f"taken{u}", align_bytes=64) for u in range(2)]
        given = keep.tile([P, 2, J], F32, name="given", align_bytes=64)
        part = [keep.tile([P, 2, J], F32, name="part", align_bytes=64)]
        pre = keep.tile([P, 2, PACK, J // 2], F32, name="pre", align_bytes=64)
        upper = keep.tile([P, 2, 2, J // 2], F32, name="upper", align_bytes=64)

        def round_w(z, u):
            src = w_raw[z][:].rearrange("p j (m t) -> p m j t", t=PACK)[:, :, :, 2 * u : 2 * u + 2]
            dst = grouped[z][:, 2 * u : 2 * u + 2].rearrange("p t m j -> p m j t")
            nc.scalar.copy(dst[:, :M_SCALAR], src[:, :M_SCALAR])
            nc.vector.tensor_copy(dst[:, M_SCALAR:], src[:, M_SCALAR:])

        def first_product(z, u):
            cols = slice(2 * u * P, 2 * (u + 1) * P)
            nc.vector.quantize_mx(out=codes[z][:, cols].bitcast(E5M2), scales=scales[z][:, cols],
                                  in_=grouped[z][:, 2 * u : 2 * u + 2].rearrange("p t m j -> p (t m j)"))
            for i in range(2):
                cols = slice((2 * u + i) * P, (2 * u + i + 1) * P)
                nc.tensor.matmul_mx(out=acc[u][:, i, :], lhsT=codes[z][:, cols].bitcast(E5M2), lhsT_scale=scales[z][:, cols],
                                    rhs=xg_words[z][:].bitcast(E4M3), rhs_scale=xg_scales[z][:],
                                    start=(z == 0 and i == 0), stop=(z == PASSES - 1 and i == 1))

        for z in range(PASSES):
            nc.vector.tensor_copy(xg_words[z][:], x_words[:, z, :].bitcast(U32).indirect(idx[:]))
        for z in range(PASSES):
            nc.vector.tensor_copy(xg_scales[z][:], x_scales[:, z, :].indirect(idx[:]))
        round_w(0, 0)
        round_w(0, 1)
        first_product(0, 0)
        first_product(0, 1)
        nc.scalar.activation(taken[0][:, 0, :], table[0][:].indirect(idx3[:]), ACT.Copy)
        nc.vector.tensor_tensor(part[0][:, 0, :], table[0][:].indirect(idx2[:]), taken[0][:, 0, :], ALU.subtract)
        nc.scalar.activation(taken[0][:, 1, :], table[1][:].indirect(idx3[:]), ACT.Copy)
        nc.vector.tensor_tensor(part[0][:, 1, :], table[1][:].indirect(idx2[:]), taken[0][:, 1, :], ALU.subtract)
        round_w(1, 1)
        round_w(1, 0)
        first_product(1, 1)
        first_product(1, 0)
        nc.scalar.activation(taken[1][:, 0, :], table[2][:].indirect(idx3[:]), ACT.Copy)
        nc.scalar.activation(given[:, 0, :], table[2][:].indirect(idx2[:]), ACT.Copy)
        nc.scalar.activation(taken[1][:, 1, :], table[3][:].indirect(idx3[:]), ACT.Copy)
        nc.vector.tensor_copy(given[:, 1, :], table[3][:].indirect(idx2[:]))

        hid = keep.tile([P, J, PACK], BF16, name="hid", align_bytes=64)
        h_codes = keep.tile([P, J], U32, name="h_codes", align_bytes=64)
        h_scales = keep.tile([P, J], U8, name="h_scales", align_bytes=64)
        halves = [slice(h * J // 2, (h + 1) * J // 2) for h in range(2)]
        for h, cols in enumerate(halves):
            nc.vector.tensor_tensor(upper[:, h], acc[1][:, :, cols], given[:, :, cols], ALU.add)
        for h, cols in enumerate(halves):
            nc.vector.tensor_tensor(pre[:, h, 0:2, :], acc[0][:, :, cols], part[0][:, :, cols], ALU.add)
        for h, cols in enumerate(halves):
            nc.vector.tensor_tensor(pre[:, h, 2:4, :], upper[:, h], taken[1][:, :, cols], ALU.subtract)
        for h, cols in enumerate(halves):
            nc.vector.tensor_scalar(hid[:, cols, :].rearrange("p (c i) t -> p c t i", i=4),
                                    pre[:, h].rearrange("p t (c i) -> p c t i", i=4), 0.0, None, ALU.max)
        for cols in halves:
            nc.vector.quantize_mx(out=h_codes[:, cols].bitcast(E5M2), scales=h_scales[:, cols],
                                  in_=hid[:, cols, :].rearrange("p j t -> p (j t)"))

        queues = [nc.sync, nc.scalar]
        for h in range(HALVES):
            prod = psum.tile([P, J], F32, name=f"prod{h}")
            nc.tensor.matmul_mx(out=prod[:], lhsT=b_words[:, 2 * P * h : 2 * P * (h + 1)].bitcast(E2M1),
                                lhsT_scale=b_scales[:, P * h : P * (h + 1)],
                                rhs=h_codes[:].bitcast(E5M2), rhs_scale=h_scales[:], start=True, stop=True)
            result = keep.tile([P, J], F32, name=f"result{h}", align_bytes=64)
            nc.vector.scalar_tensor_tensor(result[:], prod[:], gain[:, h, :], res[:, h, :], ALU.mult, ALU.add)
            queues[h].dma_start(out=out[P * h : P * (h + 1), :], in_=result[:])
